import numpy as np
import ml_dtypes


def mxq(x, axis, fmt="e4m3"):
    dtype, down = {"e4m3": (ml_dtypes.float8_e4m3fn, 7), "e5m2": (ml_dtypes.float8_e5m2, 14)}[fmt]
    v = np.moveaxis(np.asarray(x, np.float32).astype(ml_dtypes.bfloat16).astype(np.float64), axis, -1)
    blocks = v.reshape(v.shape[:-1] + (-1, 32))
    amax = np.abs(blocks).max(-1, keepdims=True)
    byte = np.maximum(np.where(amax > 0, np.frexp(amax)[1] - 1 + 127, 0) - down, 1)
    scale = np.exp2(byte - 127.0)
    codes = (blocks / scale).astype(np.float32).astype(dtype).astype(np.float64)
    return np.moveaxis((codes * scale).reshape(v.shape), -1, axis)


WIDE = False


def mx_kscale(k):
    if not WIDE:
        return np.ones(k)
    levels = np.array([10, -10, 5, -5, 0])
    if k % 512:
        return np.exp2(np.random.permutation(np.resize(levels, k // 32))).repeat(32)
    a = np.empty((k // 512, 16))
    for p in range(k // 512):
        a[p, :8] = np.random.permutation(np.resize(levels, 8))
        for g in range(8):
            far = levels[np.abs(levels - a[p, g]) >= 10]
            a[p, g + 8] = far[np.random.randint(len(far))]
    return np.exp2(a.ravel()).repeat(32)


BF16 = ml_dtypes.bfloat16


def bf(x):
    return np.asarray(x, np.float32).astype(BF16)


def f64(x):
    return np.asarray(x).astype(np.float64)


E2M1 = np.array([0.0, 0.5, 1.0, 1.5, 2.0, 3.0, 4.0, 6.0, -0.0, -0.5, -1.0, -1.5, -2.0, -3.0, -4.0, -6.0])


def pack_weight(w, fmt):
    k, n = w.shape
    w = f64(bf(w)).reshape(k // 32, 32, n)
    amax = np.abs(w).max(1)
    if fmt == "e4m3":
        byte = np.frexp(amax)[1] - 1 + 127 - 7
    else:
        mant, ex = np.frexp(amax / 6.0)
        byte = np.where(mant > 0.5, ex, ex - 1) + 127
    byte = np.clip(np.where(amax > 0, byte, 1), 1, 254)
    scaled = (w * np.exp2(127.0 - byte)[:, None, :]).reshape(k, n).astype(np.float32)
    by_word = np.ascontiguousarray(scaled.reshape(k // 512, 128, 4, n).transpose(0, 1, 3, 2))
    if fmt == "e4m3":
        words = by_word.astype(ml_dtypes.float8_e4m3fn).view(np.uint8)
    else:
        c = by_word.astype(ml_dtypes.float4_e2m1fn).view(np.uint8) & 0xF
        words = c[..., 0::2] | (c[..., 1::2] << 4)
    return np.ascontiguousarray(words), np.ascontiguousarray(byte.astype(np.uint8).reshape(k // 512, 16, n))


def unpack_weight(words, scales, fmt):
    g, p, n, _ = words.shape
    if fmt == "e4m3":
        vals = np.ascontiguousarray(words).view(ml_dtypes.float8_e4m3fn).astype(np.float64)
    else:
        nib = np.empty((g, p, n, 4), np.uint8)
        nib[..., 0::2] = words & 0xF
        nib[..., 1::2] = words >> 4
        vals = E2M1[nib]
    vals = vals * np.repeat(np.exp2(scales.astype(np.float64) - 127.0), 8, axis=1)[..., None]
    return vals.transpose(0, 1, 3, 2).reshape(g * 512, n)
def pack4(w):
    words, scales = pack_weight(w, "e2m1")
    return words.reshape(words.shape[0], 128, -1), scales


def unpack4(words, scales):
    return unpack_weight(words.reshape(words.shape[0], 128, -1, 2), scales, "e2m1")


M, K, D, N = 1024, 2048, 1024, 2048


def setup_inputs():
    s = mx_kscale(K)
    t = mx_kscale(D)
    fp = np.random.standard_normal((K, M)) * s[:, None]
    metric = np.random.standard_normal((K, D)) / np.sqrt(K) / s[:, None] * t
    fp_words, fp_scales = pack4(fp)
    metric_words, metric_scales = pack4(metric)
    return {"fp_words": fp_words,
            "fp_scales": fp_scales,
            "metric_words": metric_words,
            "metric_scales": metric_scales,
            "shift": bf(0.3 * np.random.standard_normal(D) * t),
            "library": bf(np.random.standard_normal((N, D)) / np.sqrt(D) / t),
            "weight": bf(1 + 0.2 * np.random.standard_normal(M)),
            "offset": bf(0.3 * np.random.standard_normal(N))}


def reference(fp_words, fp_scales, metric_words, metric_scales, shift, library, weight, offset):
    fp = unpack4(fp_words, fp_scales)
    metric = unpack4(metric_words, metric_scales)
    h = fp.T @ metric
    h = np.maximum(h + f64(shift), 0.0)
    hq = mxq(h, 1, "e4m3")
    lq = mxq(f64(library), 1, "e4m3")
    scores = hq @ lq.T
    return scores * f64(weight)[:, None] + f64(offset)

@@ -1,0 +1,260 @@
+from contextlib import ExitStack
+
+import concourse.mybir as mybir
+from concourse.masks import make_identity
+
+M, K, D, N = 1024, 2048, 1024, 2048
+FLOPS = 2 * M * K * D + 2 * M * D * N
+
+F32 = mybir.dt.float32
+BF16 = mybir.dt.bfloat16
+I32 = mybir.dt.int32
+U32 = mybir.dt.uint32
+U8 = mybir.dt.uint8
+FP4X4 = mybir.dt.float4_e2m1fn_x4
+FP8X4 = mybir.dt.float8_e4m3fn_x4
+ADD = mybir.AluOpType.add
+MULT = mybir.AluOpType.mult
+MAX = mybir.AluOpType.max
+ACT = mybir.ActivationFunctionType
+
+P = 128
+KG = K // 512
+DG = D // 512
+W = 512
+MI = W // P
+NJ = N // W
+
+
+def tile_molecule_embedding_scores_s4_kernel(
+    tc, fp_words, fp_scales, metric_words, metric_scales, shift, library, weight, offset, out
+):
+    nc = tc.nc
+    with ExitStack() as ctx:
+        keep = ctx.enter_context(tc.tile_pool(name="keep", bufs=1))
+        stage = ctx.enter_context(tc.tile_pool(name="stage", bufs=8))
+        psum = ctx.enter_context(tc.psum_pool(name="psum", bufs=8))
+        ctx.enter_context(tc.manual_schedule())
+
+        m_raw = keep.tile([P, KG, 2 * D], U8, align_bytes=64, name="m_raw")
+        m_cod = keep.tile([P, KG, DG, 4, 2 * P], U8, align_bytes=64, name="m_cod")
+        ms_raw = keep.tile([P, KG, D], U8, align_bytes=64, name="ms_raw")
+        ms_cod = keep.tile([P, KG, DG, 4, P], U8, align_bytes=64, name="ms_cod")
+        f_cod = keep.tile([P, KG, 2 * M], U8, align_bytes=64, name="f_cod")
+        f_scl = keep.tile([P, KG, M], U8, align_bytes=64, name="f_scl")
+        sh = keep.tile([P, DG, 4], BF16, name="sh")
+        sh_f = keep.tile([P, DG, 4], F32, name="sh_f")
+        w_row = keep.tile([P, P], BF16, name="w_row")
+        w_f32 = keep.tile([P, P], F32, name="w_f32")
+        w_col = keep.tile([P, M // P], F32, name="w_col")
+        off = keep.tile([P, N], BF16, name="off")
+        ident = keep.tile([P, P], F32, name="ident")
+        warm = keep.tile([P, 1], F32, name="warm")
+
+        l_raw = [keep.tile([P, MI, D], BF16, align_bytes=64, name=f"l_raw{j}") for j in range(NJ)]
+        l_grp = {}
+        l_cod = {}
+        l_scl = {}
+        for j in range(NJ):
+            for g in range(DG):
+                l_grp[j, g] = keep.tile([P, 4 * W], BF16, align_bytes=64, name=f"l_grp{j}{g}")
+                l_cod[j, g] = keep.tile([P, W], U32, align_bytes=64, name=f"l_cod{j}{g}")
+                l_scl[j, g] = keep.tile([P, W], U8, align_bytes=64, name=f"l_scl{j}{g}")
+        h_raw = {}
+        h_grp = {}
+        h_cod = {}
+        h_scl = {}
+        for h in range(2):
+            for g in range(DG):
+                h_raw[h, g] = keep.tile([P, 4, W], BF16, align_bytes=64, name=f"h_raw{h}{g}")
+                h_grp[h, g] = keep.tile([P, 4 * W], BF16, align_bytes=64, name=f"h_grp{h}{g}")
+                h_cod[h, g] = keep.tile([P, W], U32, align_bytes=64, name=f"h_cod{h}{g}")
+                h_scl[h, g] = keep.tile([P, W], U8, align_bytes=64, name=f"h_scl{h}{g}")
+
+        nc.gpsimd.memset(ms_raw[:].bitcast(I32), 0)
+        nc.gpsimd.memset(f_scl[:].bitcast(I32), 0)
+        nc.gpsimd.memset(warm[:], 0.0)
+        nc.scalar.activation(out=warm[:], in_=warm[:], func=ACT.Relu)
+        nc.gpsimd.memset(w_row[:], 0.0)
+
+        ms_src = metric_scales.bitcast(I32).rearrange("g (q r) n -> r q g n", r=4)
+        fs_src = fp_scales.bitcast(I32).rearrange("g (q r) n -> r q g n", r=4)
+        fa = fp_words.rearrange("g p w -> p g w")
+        ma = metric_words.rearrange("g p w -> p g w")
+        nc.sync.dma_start(out=m_raw[:, 0, :], in_=ma[:, 0, :])
+        nc.sync.dma_start(out=f_cod[:, 0, 0:1024], in_=fa[:, 0, 0:1024])
+        for r in range(4):
+            nc.sync.dma_start(out=ms_raw[:].bitcast(I32)[r:P:32], in_=ms_src[r])
+        for r in range(4):
+            q = nc.sync
+            q.dma_start(out=f_scl[:].bitcast(I32)[r:P:32], in_=fs_src[r])
+        nc.sync.dma_start(out=m_raw[:, 1, :], in_=ma[:, 1, :])
+        nc.sync.dma_start(out=f_cod[:, 1:4, 0:1024], in_=fa[:, 1:4, 0:1024])
+        nc.sync.dma_start(out=m_raw[:, 2:4, :], in_=ma[:, 2:4, :])
+        nc.sync.dma_start(out=sh[:], in_=shift.rearrange("(g p t) -> p g t", p=P, t=4))
+        nc.sync.dma_start(out=w_row[0 : M // P, :], in_=weight.rearrange("(c p) -> c p", p=P))
+        nc.sync.dma_start(out=f_cod[:, :, 1024:2048], in_=fa[:, :, 1024:2048])
+        for j in range(NJ):
+            src = library[j * W : (j + 1) * W, :].rearrange("(a p) k -> p a k", p=P)
+            if j == 3:
+                nc.sync.dma_start(out=off[:], in_=offset.partition_broadcast(P))
+            for a in range(0, MI, 2):
+                nc.sync.dma_start(out=l_raw[j][:, a : a + 2, :], in_=src[:, a : a + 2, :])
+        make_identity(nc, ident[:])
+
+        def permute(gs, ds):
+            for g in gs:
+                nc.vector.tensor_copy(
+                    out=m_cod[:, g, ds].rearrange("p d t (q b) -> p d t q b", b=2),
+                    in_=m_raw[:, g, :].rearrange("p (d q t b) -> p d t q b", d=DG, t=4, b=2)[:, ds],
+                )
+                nc.vector.tensor_copy(
+                    out=ms_cod[:, g, ds],
+                    in_=ms_raw[:, g, :].rearrange("p (d q t) -> p d t q", d=DG, t=4)[:, ds],
+                )
+
+        def s1(bank, h, d, t, g):
+            nc.tensor.matmul_mx(
+                out=bank[:],
+                lhsT=m_cod[:, g, d, t, :].bitcast(FP4X4),
+                lhsT_scale=ms_cod[:, g, d, t, :],
+                rhs=f_cod[:, g, 1024 * h : 1024 * (h + 1)].bitcast(FP4X4),
+                rhs_scale=f_scl[:, g, 512 * h : 512 * (h + 1)],
+                start=(g == 0),
+                stop=(g == KG - 1),
+            )
+
+        def h_out(bank, h, d, t, eng):
+            if eng == "S":
+                nc.scalar.activation(out=h_raw[h, d][:, t, :], in_=bank[:], func=ACT.Relu, bias=sh[:, d, t : t + 1])
+            else:
+                nc.vector.tensor_scalar(
+                    out=h_raw[h, d][:, t, :], in0=bank[:], scalar1=sh_f[:, d, t : t + 1], scalar2=0.0, op0=ADD, op1=MAX
+                )
+
+        def h_interleave(h, d):
+            nc.vector.tensor_copy(
+                out=h_grp[h, d][:].rearrange("p (m t) -> p m t", t=4), in_=h_raw[h, d][:].rearrange("p t m -> p m t")
+            )
+
+        def h_quant(h, d):
+            nc.vector.quantize_mx(out=h_cod[h, d][:].bitcast(FP8X4), scales=h_scl[h, d][:], in_=h_grp[h, d][:])
+
+        def l_quant(j, g):
+            nc.vector.quantize_mx(out=l_cod[j, g][:].bitcast(FP8X4), scales=l_scl[j, g][:], in_=l_grp[j, g][:])
+
+        def s1_whole(h, d, t):
+            bank = psum.tile([P, W], F32, name="bank", tag="bank")
+            for g in range(KG):
+                s1(bank, h, d, t, g)
+            h_out(bank, h, d, t, "S")
+
+        def l_turn(j):
+            for a in range(0, MI, 2):
+                for g in range(DG):
+                    bank = psum.tile([P, W], F32, name="bank", tag="bank")
+                    for i in range(2):
+                        words = l_raw[j][:, a + i, :].bitcast(F32)
+                        for u in range(2):
+                            c = (2 * i + u) * P
+                            nc.tensor.transpose(
+                                bank[:, c : c + P], words[:, 256 * g + u : 256 * (g + 1) : 2], ident[:]
+                            )
+                    nc.scalar.copy(
+                        out=l_grp[j, g][:].bitcast(F32)[:, 256 * a : 256 * a + 512].rearrange(
+                            "p (a r u) -> p a r u", a=2, u=2
+                        ),
+                        in_=bank[:].rearrange("p (a u r) -> p a r u", a=2, u=2),
+                    )
+
+        def s2(h, j, i, path):
+            bank = psum.tile([P, W], F32, name="bank", tag="bank")
+            for g in range(DG):
+                nc.tensor.matmul_mx(
+                    out=bank[:],
+                    lhsT=h_cod[h, g][:, P * i : P * (i + 1)].bitcast(FP8X4),
+                    lhsT_scale=h_scl[h, g][:, P * i : P * (i + 1)],
+                    rhs=l_cod[j, g][:].bitcast(FP8X4),
+                    rhs_scale=l_scl[j, g][:],
+                    start=(g == 0),
+                    stop=(g == DG - 1),
+                )
+            res = stage.tile([P, W], F32, name="res", tag="res")
+            c = MI * h + i
+            cols = slice(W * j, W * (j + 1))
+            if path == "V":
+                nc.vector.scalar_tensor_tensor(
+                    out=res[:], in0=bank[:], scalar=w_col[:, c : c + 1], in1=off[:, cols], op0=MULT, op1=ADD
+                )
+            else:
+                tmp = stage.tile([P, W], F32, name="tmp", tag="tmp", bufs=3)
+                nc.scalar.activation(out=tmp[:], in_=bank[:], func=ACT.Copy, scale=w_col[:, c : c + 1])
+                nc.gpsimd.tensor_tensor(out=res[:], in0=tmp[:], in1=off[:, cols], op=ADD)
+            nc.sync.dma_start(out=out[P * c : P * (c + 1), cols], in_=res[:])
+
+        banks = {}
+        for d in range(DG):
+            for t in range(4):
+                banks[d, t] = psum.tile([P, W], F32, name="bank", tag="bank")
+        for g in range(KG):
+            if g == 0:
+                permute([0], slice(0, 1))
+                permute([0], slice(1, 2))
+            else:
+                permute([g], slice(0, 2))
+            for d in range(DG):
+                for t in range(4):
+                    s1(banks[d, t], 0, d, t, g)
+        nc.vector.tensor_copy(out=sh_f[:], in_=sh[:])
+        nc.vector.tensor_copy(out=w_f32[:], in_=w_row[:])
+        for d in range(DG):
+            for t in range(4):
+                h_out(banks[d, t], 0, d, t, "SV"[t % 2])
+
+        bank = psum.tile([P, W], F32, name="bank", tag="bank")
+        nc.tensor.transpose(bank[:, 0:P], w_f32[:], ident[:])
+        nc.scalar.copy(out=w_col[:], in_=bank[:, 0 : M // P])
+        h_interleave(0, 0)
+        h_interleave(0, 1)
+        h_quant(0, 0)
+        h_quant(0, 1)
+        l_turn(0)
+        l_quant(0, 0)
+        l_quant(0, 1)
+        for t in range(3):
+            s1_whole(1, 0, t)
+        for i in range(MI):
+            s2(0, 0, i, "V")
+        s1_whole(1, 0, 3)
+        l_turn(1)
+        h_interleave(1, 0)
+        l_quant(1, 0)
+        l_quant(1, 1)
+        h_quant(1, 0)
+        for t in range(4):
+            s1_whole(1, 1, t)
+        s2(0, 1, 0, "V")
+        h_interleave(1, 1)
+        s2(0, 1, 1, "V")
+        h_quant(1, 1)
+        s2(0, 1, 2, "V")
+        s2(0, 1, 3, "V")
+        l_turn(2)
+        s2(1, 0, 0, "V")
+        s2(1, 0, 1, "V")
+        l_quant(2, 0)
+        s2(1, 0, 2, "V")
+        l_quant(2, 1)
+        s2(1, 0, 3, "V")
+        for i in range(MI):
+            s2(1, 1, i, "V")
+        l_turn(3)
+        s2(0, 2, 0, "V")
+        s2(0, 2, 1, "V")
+        l_quant(3, 0)
+        l_quant(3, 1)
+        s2(0, 2, 2, "S")
+        s2(0, 2, 3, "V")
+        for h, j in ((1, 2), (0, 3), (1, 3)):
+            for i in range(MI):
+                s2(h, j, i, "S" if i == 1 else "V")

@@ -52,6 +52,7 @@ def tile_molecule_embedding_scores_s4_kernel(
         warm = keep.tile([P, 1], F32, name="warm")
 
         l_raw = [keep.tile([P, MI, D], BF16, align_bytes=64, name=f"l_raw{j}") for j in range(NJ)]
+        l_spl = [keep.tile([P, MI, D // 2], F32, align_bytes=64, name=f"l_spl{j}") for j in range(NJ)]
         l_grp = {}
         l_cod = {}
         l_scl = {}
@@ -71,47 +72,59 @@ def tile_molecule_embedding_scores_s4_kernel(
                 h_cod[h, g] = keep.tile([P, W], U32, align_bytes=64, name=f"h_cod{h}{g}")
                 h_scl[h, g] = keep.tile([P, W], U8, align_bytes=64, name=f"h_scl{h}{g}")
 
-        nc.gpsimd.memset(ms_raw[:].bitcast(I32), 0)
-        nc.gpsimd.memset(f_scl[:].bitcast(I32), 0)
-        nc.gpsimd.memset(warm[:], 0.0)
-        nc.scalar.activation(out=warm[:], in_=warm[:], func=ACT.Relu)
-        nc.gpsimd.memset(w_row[:], 0.0)
+        def scales(dst, src, gs, cols):
+            rows = src.bitcast(I32).rearrange("g (q r) n -> r q g n", r=4)
+            for r in range(4):
+                nc.sync.dma_start(out=dst[:].bitcast(I32)[r:P:32, gs, cols], in_=rows[r][:, gs, cols])
 
-        ms_src = metric_scales.bitcast(I32).rearrange("g (q r) n -> r q g n", r=4)
-        fs_src = fp_scales.bitcast(I32).rearrange("g (q r) n -> r q g n", r=4)
         fa = fp_words.rearrange("g p w -> p g w")
         ma = metric_words.rearrange("g p w -> p g w")
-        nc.sync.dma_start(out=m_raw[:, 0, :], in_=ma[:, 0, :])
+        lib = library.rearrange("(j a p) k -> j p a k", a=MI, p=P)
+        early = slice(0, 2)
+        late = slice(2, KG)
+        qa = slice(0, W // 4)
+        qb = slice(W // 4, M // 4)
+        for gs in (early, late):
+            nc.vector.memset(ms_raw[:].bitcast(I32)[:, gs], 0)
+            nc.vector.memset(f_scl[:].bitcast(I32)[:, gs], 0)
+        nc.vector.memset(warm[:], 0.0)
+        nc.scalar.activation(out=warm[:], in_=warm[:], func=ACT.Relu)
+        make_identity(nc, ident[:])
+        nc.gpsimd.memset(w_row[:], 0.0)
+        nc.sync.dma_start(out=m_raw[:, 0], in_=ma[:, 0])
         nc.sync.dma_start(out=f_cod[:, 0, 0:1024], in_=fa[:, 0, 0:1024])
-        for r in range(4):
-            nc.sync.dma_start(out=ms_raw[:].bitcast(I32)[r:P:32], in_=ms_src[r])
-        for r in range(4):
-            q = nc.sync
-            q.dma_start(out=f_scl[:].bitcast(I32)[r:P:32], in_=fs_src[r])
+        scales(ms_raw, metric_scales, early, slice(0, D // 4))
+        scales(f_scl, fp_scales, early, qa)
         nc.sync.dma_start(out=m_raw[:, 1, :], in_=ma[:, 1, :])
         nc.sync.dma_start(out=f_cod[:, 1:4, 0:1024], in_=fa[:, 1:4, 0:1024])
+        scales(ms_raw, metric_scales, late, slice(0, D // 4))
         nc.sync.dma_start(out=m_raw[:, 2:4, :], in_=ma[:, 2:4, :])
+        scales(f_scl, fp_scales, late, qa)
         nc.sync.dma_start(out=sh[:], in_=shift.rearrange("(g p t) -> p g t", p=P, t=4))
         nc.sync.dma_start(out=w_row[0 : M // P, :], in_=weight.rearrange("(c p) -> c p", p=P))
-        nc.sync.dma_start(out=f_cod[:, :, 1024:2048], in_=fa[:, :, 1024:2048])
         for j in range(NJ):
-            src = library[j * W : (j + 1) * W, :].rearrange("(a p) k -> p a k", p=P)
+            if j == 1:
+                scales(f_scl, fp_scales, slice(0, KG), qb)
+                nc.sync.dma_start(out=f_cod[:, :, 1024:2048], in_=fa[:, :, 1024:2048])
             if j == 3:
                 nc.sync.dma_start(out=off[:], in_=offset.partition_broadcast(P))
             for a in range(0, MI, 2):
-                nc.sync.dma_start(out=l_raw[j][:, a : a + 2, :], in_=src[:, a : a + 2, :])
-        make_identity(nc, ident[:])
+                nc.sync.dma_start(out=l_raw[j][:, a : a + 2, :], in_=lib[j, :, a : a + 2, :])
 
-        def permute(gs, ds):
-            for g in gs:
-                nc.vector.tensor_copy(
-                    out=m_cod[:, g, ds].rearrange("p d t (q b) -> p d t q b", b=2),
-                    in_=m_raw[:, g, :].rearrange("p (d q t b) -> p d t q b", d=DG, t=4, b=2)[:, ds],
-                )
-                nc.vector.tensor_copy(
-                    out=ms_cod[:, g, ds],
-                    in_=ms_raw[:, g, :].rearrange("p (d q t) -> p d t q", d=DG, t=4)[:, ds],
-                )
+        def l_split(j, a):
+            nc.scalar.copy(
+                out=l_spl[j][:, a : a + 2, :].rearrange("p a (g u q) -> p (a g) u q", g=DG, u=2),
+                in_=l_raw[j][:, a : a + 2, :].bitcast(F32).rearrange("p a (g q u) -> p (a g) u q", g=DG, u=2),
+            )
+
+        def permute(g, d):
+            nc.vector.tensor_copy(
+                out=m_cod[:, g, d].rearrange("p t (q b) -> p t q b", b=2),
+                in_=m_raw[:, g, :].rearrange("p (d q t b) -> p d t q b", d=DG, t=4, b=2)[:, d],
+            )
+            nc.vector.tensor_copy(
+                out=ms_cod[:, g, d], in_=ms_raw[:, g, :].rearrange("p (d q t) -> p d t q", d=DG, t=4)[:, d]
+            )
 
         def s1(bank, h, d, t, g):
             nc.tensor.matmul_mx(
@@ -154,12 +167,10 @@ def tile_molecule_embedding_scores_s4_kernel(
                 for g in range(DG):
                     bank = psum.tile([P, W], F32, name="bank", tag="bank")
                     for i in range(2):
-                        words = l_raw[j][:, a + i, :].bitcast(F32)
                         for u in range(2):
                             c = (2 * i + u) * P
-                            nc.tensor.transpose(
-                                bank[:, c : c + P], words[:, 256 * g + u : 256 * (g + 1) : 2], ident[:]
-                            )
+                            k0 = (2 * g + u) * P
+                            nc.tensor.transpose(bank[:, c : c + P], l_spl[j][:, a + i, k0 : k0 + P], ident[:])
                     nc.scalar.copy(
                         out=l_grp[j, g][:].bitcast(F32)[:, 256 * a : 256 * a + 512].rearrange(
                             "p (a r u) -> p a r u", a=2, u=2
@@ -186,6 +197,15 @@ def tile_molecule_embedding_scores_s4_kernel(
                 nc.vector.scalar_tensor_tensor(
                     out=res[:], in0=bank[:], scalar=w_col[:, c : c + 1], in1=off[:, cols], op0=MULT, op1=ADD
                 )
+            elif path == "V2":
+                for n in (0, W // 2):
+                    half = slice(n, n + W // 2)
+                    part = slice(W * j + n, W * j + n + W // 2)
+                    nc.vector.scalar_tensor_tensor(
+                        out=res[:, half], in0=bank[:, half], scalar=w_col[:, c : c + 1], in1=off[:, part], op0=MULT, op1=ADD
+                    )
+                    nc.sync.dma_start(out=out[P * c : P * (c + 1), part], in_=res[:, half])
+                return
             else:
                 tmp = stage.tile([P, W], F32, name="tmp", tag="tmp", bufs=3)
                 nc.scalar.activation(out=tmp[:], in_=bank[:], func=ACT.Copy, scale=w_col[:, c : c + 1])
@@ -197,16 +217,15 @@ def tile_molecule_embedding_scores_s4_kernel(
             for t in range(4):
                 banks[d, t] = psum.tile([P, W], F32, name="bank", tag="bank")
         for g in range(KG):
-            if g == 0:
-                permute([0], slice(0, 1))
-                permute([0], slice(1, 2))
-            else:
-                permute([g], slice(0, 2))
+            permute(g, 0)
+            permute(g, 1)
             for d in range(DG):
                 for t in range(4):
                     s1(banks[d, t], 0, d, t, g)
         nc.vector.tensor_copy(out=sh_f[:], in_=sh[:])
         nc.vector.tensor_copy(out=w_f32[:], in_=w_row[:])
+        l_split(0, 0)
+        l_split(0, 2)
         for d in range(DG):
             for t in range(4):
                 h_out(banks[d, t], 0, d, t, "SV"[t % 2])
@@ -221,8 +240,11 @@ def tile_molecule_embedding_scores_s4_kernel(
         l_turn(0)
         l_quant(0, 0)
         l_quant(0, 1)
-        for t in range(3):
-            s1_whole(1, 0, t)
+        s1_whole(1, 0, 0)
+        l_split(1, 0)
+        s1_whole(1, 0, 1)
+        l_split(1, 2)
+        s1_whole(1, 0, 2)
         for i in range(MI):
             s2(0, 0, i, "V")
         s1_whole(1, 0, 3)
@@ -233,6 +255,8 @@ def tile_molecule_embedding_scores_s4_kernel(
         h_quant(1, 0)
         for t in range(4):
             s1_whole(1, 1, t)
+        l_split(2, 0)
+        l_split(2, 2)
         s2(0, 1, 0, "V")
         h_interleave(1, 1)
         s2(0, 1, 1, "V")
@@ -240,6 +264,8 @@ def tile_molecule_embedding_scores_s4_kernel(
         s2(0, 1, 2, "V")
         s2(0, 1, 3, "V")
         l_turn(2)
+        l_split(3, 0)
+        l_split(3, 2)
         s2(1, 0, 0, "V")
         s2(1, 0, 1, "V")
         l_quant(2, 0)
@@ -257,4 +283,4 @@ def tile_molecule_embedding_scores_s4_kernel(
         s2(0, 2, 3, "V")
         for h, j in ((1, 2), (0, 3), (1, 3)):
             for i in range(MI):
-                s2(h, j, i, "S" if i == 1 else "V")
+                s2(h, j, i, "S" if i == 1 else "V2" if (h, j, i) == (1, 3, 3) else "V")

@@ -32,14 +32,14 @@ def tile_molecule_embedding_scores_s4_kernel(
     nc = tc.nc
     with ExitStack() as ctx:
         keep = ctx.enter_context(tc.tile_pool(name="keep", bufs=1))
-        stage = ctx.enter_context(tc.tile_pool(name="stage", bufs=8))
+        stage = ctx.enter_context(tc.tile_pool(name="stage", bufs=12))
         psum = ctx.enter_context(tc.psum_pool(name="psum", bufs=8))
         ctx.enter_context(tc.manual_schedule())
 
-        m_raw = keep.tile([P, KG, 2 * D], U8, align_bytes=64, name="m_raw")
-        m_cod = keep.tile([P, KG, DG, 4, 2 * P], U8, align_bytes=64, name="m_cod")
-        ms_raw = keep.tile([P, KG, D], U8, align_bytes=64, name="ms_raw")
-        ms_cod = keep.tile([P, KG, DG, 4, P], U8, align_bytes=64, name="ms_cod")
+        m_raw = [keep.tile([P, KG, D], U8, align_bytes=64, name=f"m_raw{d}") for d in range(DG)]
+        m_cod = [keep.tile([P, KG, 4, 2 * P], U8, align_bytes=64, name=f"m_cod{d}") for d in range(DG)]
+        ms_raw = [keep.tile([P, KG, W], U8, align_bytes=64, name=f"ms_raw{d}") for d in range(DG)]
+        ms_cod = [keep.tile([P, KG, 4, P], U8, align_bytes=64, name=f"ms_cod{d}") for d in range(DG)]
         f_cod = keep.tile([P, KG, 2 * M], U8, align_bytes=64, name="f_cod")
         f_scl = keep.tile([P, KG, M], U8, align_bytes=64, name="f_scl")
         sh = keep.tile([P, DG, 4], BF16, name="sh")
@@ -51,8 +51,8 @@ def tile_molecule_embedding_scores_s4_kernel(
         ident = keep.tile([P, P], F32, name="ident")
         warm = keep.tile([P, 1], F32, name="warm")
 
-        l_raw = [keep.tile([P, MI, D], BF16, align_bytes=64, name=f"l_raw{j}") for j in range(NJ)]
-        l_spl = [keep.tile([P, MI, D // 2], F32, align_bytes=64, name=f"l_spl{j}") for j in range(NJ)]
+        l_raw = [[keep.tile([P, 2, D], BF16, align_bytes=64, name=f"l_raw{j}{b}") for b in range(2)] for j in range(NJ)]
+        l_spl = [[keep.tile([P, 2, D // 2], F32, align_bytes=64, name=f"l_spl{j}{b}") for b in range(2)] for j in range(NJ)]
         l_grp = {}
         l_cod = {}
         l_scl = {}
@@ -72,65 +72,63 @@ def tile_molecule_embedding_scores_s4_kernel(
                 h_cod[h, g] = keep.tile([P, W], U32, align_bytes=64, name=f"h_cod{h}{g}")
                 h_scl[h, g] = keep.tile([P, W], U8, align_bytes=64, name=f"h_scl{h}{g}")
 
-        def scales(dst, src, gs, cols):
-            rows = src.bitcast(I32).rearrange("g (q r) n -> r q g n", r=4)
+        def scales(dst, src):
+            rows = src.rearrange("g (q r) n -> r q g n", r=4)
             for r in range(4):
-                nc.sync.dma_start(out=dst[:].bitcast(I32)[r:P:32, gs, cols], in_=rows[r][:, gs, cols])
+                nc.sync.dma_start(out=dst[:].bitcast(I32)[r:P:32], in_=rows[r])
+
+        mi = metric_scales.bitcast(I32)
+        mi = [mi[:, :, W // 4 * d : W // 4 * (d + 1)] for d in range(DG)]
 
         fa = fp_words.rearrange("g p w -> p g w")
-        ma = metric_words.rearrange("g p w -> p g w")
-        lib = library.rearrange("(j a p) k -> j p a k", a=MI, p=P)
-        early = slice(0, 2)
-        late = slice(2, KG)
-        qa = slice(0, W // 4)
-        qb = slice(W // 4, M // 4)
-        for gs in (early, late):
-            nc.vector.memset(ms_raw[:].bitcast(I32)[:, gs], 0)
-            nc.vector.memset(f_scl[:].bitcast(I32)[:, gs], 0)
+        ma = metric_words.rearrange("g p (d w) -> d p g w", d=DG)
+        lib = library.rearrange("(j b a p) k -> j b p a k", b=2, a=2, p=P)
+        nc.gpsimd.dma_start(out=f_cod[:].bitcast(I32)[:, 0], in_=fa.bitcast(I32)[:, 0])
+        nc.vector.memset(ms_raw[0][:].bitcast(I32), 0)
+        nc.vector.memset(f_scl[:].bitcast(I32), 0)
+        nc.vector.memset(ms_raw[1][:].bitcast(I32), 0)
         nc.vector.memset(warm[:], 0.0)
         nc.scalar.activation(out=warm[:], in_=warm[:], func=ACT.Relu)
         make_identity(nc, ident[:])
         nc.gpsimd.memset(w_row[:], 0.0)
-        nc.sync.dma_start(out=m_raw[:, 0], in_=ma[:, 0])
-        nc.sync.dma_start(out=f_cod[:, 0, 0:1024], in_=fa[:, 0, 0:1024])
-        scales(ms_raw, metric_scales, early, slice(0, D // 4))
-        scales(f_scl, fp_scales, early, qa)
-        nc.sync.dma_start(out=m_raw[:, 1, :], in_=ma[:, 1, :])
-        nc.sync.dma_start(out=f_cod[:, 1:4, 0:1024], in_=fa[:, 1:4, 0:1024])
-        scales(ms_raw, metric_scales, late, slice(0, D // 4))
-        nc.sync.dma_start(out=m_raw[:, 2:4, :], in_=ma[:, 2:4, :])
-        scales(f_scl, fp_scales, late, qa)
+        nc.sync.dma_start(out=m_raw[0][:, 0], in_=ma[0][:, 0])
+        scales(ms_raw[0], mi[0])
+        scales(f_scl, fp_scales.bitcast(I32))
+        nc.sync.dma_start(out=m_raw[0][:, 1], in_=ma[0][:, 1])
+        nc.sync.dma_start(out=f_cod[:, 1], in_=fa[:, 1])
+        nc.sync.dma_start(out=m_raw[0][:, 2:4], in_=ma[0][:, 2:4])
+        nc.sync.dma_start(out=f_cod[:, 2:4], in_=fa[:, 2:4])
+        nc.sync.dma_start(out=m_raw[1][:], in_=ma[1])
+        scales(ms_raw[1], mi[1])
         nc.sync.dma_start(out=sh[:], in_=shift.rearrange("(g p t) -> p g t", p=P, t=4))
         nc.sync.dma_start(out=w_row[0 : M // P, :], in_=weight.rearrange("(c p) -> c p", p=P))
         for j in range(NJ):
-            if j == 1:
-                scales(f_scl, fp_scales, slice(0, KG), qb)
-                nc.sync.dma_start(out=f_cod[:, :, 1024:2048], in_=fa[:, :, 1024:2048])
-            if j == 3:
-                nc.sync.dma_start(out=off[:], in_=offset.partition_broadcast(P))
-            for a in range(0, MI, 2):
-                nc.sync.dma_start(out=l_raw[j][:, a : a + 2, :], in_=lib[j, :, a : a + 2, :])
+            for b in range(2):
+                nc.sync.dma_start(out=l_raw[j][b][:], in_=lib[j, b])
+        nc.sync.dma_start(out=off[:], in_=offset.partition_broadcast(P))
 
-        def l_split(j, a):
+        nc.gpsimd.tensor_copy(out=w_f32[:], in_=w_row[:])
+
+        def l_split(j, b):
             nc.scalar.copy(
-                out=l_spl[j][:, a : a + 2, :].rearrange("p a (g u q) -> p (a g) u q", g=DG, u=2),
-                in_=l_raw[j][:, a : a + 2, :].bitcast(F32).rearrange("p a (g q u) -> p (a g) u q", g=DG, u=2),
+                out=l_spl[j][b][:].rearrange("p a (g u q) -> p (a g) u q", g=DG, u=2),
+                in_=l_raw[j][b][:].bitcast(F32).rearrange("p a (g q u) -> p (a g) u q", g=DG, u=2),
             )
 
-        def permute(g, d):
+        def words_in_order(g, d):
             nc.vector.tensor_copy(
-                out=m_cod[:, g, d].rearrange("p t (q b) -> p t q b", b=2),
-                in_=m_raw[:, g, :].rearrange("p (d q t b) -> p d t q b", d=DG, t=4, b=2)[:, d],
+                out=m_cod[d][:, g].rearrange("p t (q b) -> p t q b", b=2),
+                in_=m_raw[d][:, g].rearrange("p (q t b) -> p t q b", t=4, b=2),
             )
-            nc.vector.tensor_copy(
-                out=ms_cod[:, g, d], in_=ms_raw[:, g, :].rearrange("p (d q t) -> p d t q", d=DG, t=4)[:, d]
-            )
+
+        def scales_in_order(g, d):
+            nc.vector.tensor_copy(out=ms_cod[d][:, g], in_=ms_raw[d][:, g].rearrange("p (q t) -> p t q", t=4))
 
         def s1(bank, h, d, t, g):
             nc.tensor.matmul_mx(
                 out=bank[:],
-                lhsT=m_cod[:, g, d, t, :].bitcast(FP4X4),
-                lhsT_scale=ms_cod[:, g, d, t, :],
+                lhsT=m_cod[d][:, g, t, :].bitcast(FP4X4),
+                lhsT_scale=ms_cod[d][:, g, t, :],
                 rhs=f_cod[:, g, 1024 * h : 1024 * (h + 1)].bitcast(FP4X4),
                 rhs_scale=f_scl[:, g, 512 * h : 512 * (h + 1)],
                 start=(g == 0),
@@ -145,10 +143,13 @@ def tile_molecule_embedding_scores_s4_kernel(
                     out=h_raw[h, d][:, t, :], in0=bank[:], scalar1=sh_f[:, d, t : t + 1], scalar2=0.0, op0=ADD, op1=MAX
                 )
 
-        def h_interleave(h, d):
-            nc.vector.tensor_copy(
-                out=h_grp[h, d][:].rearrange("p (m t) -> p m t", t=4), in_=h_raw[h, d][:].rearrange("p t m -> p m t")
-            )
+        def h_interleave(h, d, vector_cols):
+            for eng, cols in ((nc.vector.tensor_copy, slice(0, vector_cols)), (nc.scalar.copy, slice(vector_cols, W))):
+                if cols.start < cols.stop:
+                    eng(
+                        out=h_grp[h, d][:, 4 * cols.start : 4 * cols.stop].rearrange("p (c i t) -> p c t i", i=4, t=4),
+                        in_=h_raw[h, d][:, :, cols].rearrange("p t (c i) -> p c t i", i=4),
+                    )
 
         def h_quant(h, d):
             nc.vector.quantize_mx(out=h_cod[h, d][:].bitcast(FP8X4), scales=h_scl[h, d][:], in_=h_grp[h, d][:])
@@ -156,29 +157,30 @@ def tile_molecule_embedding_scores_s4_kernel(
         def l_quant(j, g):
             nc.vector.quantize_mx(out=l_cod[j, g][:].bitcast(FP8X4), scales=l_scl[j, g][:], in_=l_grp[j, g][:])
 
-        def s1_whole(h, d, t):
+        def s1_whole(h, d, t, eng):
             bank = psum.tile([P, W], F32, name="bank", tag="bank")
             for g in range(KG):
                 s1(bank, h, d, t, g)
-            h_out(bank, h, d, t, "S")
+            h_out(bank, h, d, t, eng)
 
-        def l_turn(j):
-            for a in range(0, MI, 2):
-                for g in range(DG):
-                    bank = psum.tile([P, W], F32, name="bank", tag="bank")
-                    for i in range(2):
-                        for u in range(2):
-                            c = (2 * i + u) * P
-                            k0 = (2 * g + u) * P
-                            nc.tensor.transpose(bank[:, c : c + P], l_spl[j][:, a + i, k0 : k0 + P], ident[:])
-                    nc.scalar.copy(
-                        out=l_grp[j, g][:].bitcast(F32)[:, 256 * a : 256 * a + 512].rearrange(
-                            "p (a r u) -> p a r u", a=2, u=2
-                        ),
-                        in_=bank[:].rearrange("p (a u r) -> p a r u", a=2, u=2),
-                    )
+        def l_turn(j, b, split, engs):
+            for g in range(DG):
+                bank = psum.tile([P, W], F32, name="bank", tag="bank")
+                for a in range(2):
+                    for u in range(2):
+                        if split:
+                            words = l_spl[j][b][:, a, (2 * g + u) * P : (2 * g + u + 1) * P]
+                        else:
+                            words = l_raw[j][b][:, a, :].bitcast(F32)[:, 256 * g + u : 256 * (g + 1) : 2]
+                        nc.tensor.transpose(bank[:, (2 * a + u) * P : (2 * a + u + 1) * P], words, ident[:])
+                dst = l_grp[j, g][:].bitcast(F32)[:, 512 * b : 512 * (b + 1)].rearrange("p (a r u) -> p a r u", a=2, u=2)
+                src = bank[:].rearrange("p (a u r) -> p a r u", a=2, u=2)
+                if engs[g] == "S":
+                    nc.scalar.copy(out=dst, in_=src)
+                else:
+                    nc.vector.tensor_copy(out=dst, in_=src)
 
-        def s2(h, j, i, path):
+        def s2(h, j, i, path="V"):
             bank = psum.tile([P, W], F32, name="bank", tag="bank")
             for g in range(DG):
                 nc.tensor.matmul_mx(
@@ -193,11 +195,7 @@ def tile_molecule_embedding_scores_s4_kernel(
             res = stage.tile([P, W], F32, name="res", tag="res")
             c = MI * h + i
             cols = slice(W * j, W * (j + 1))
-            if path == "V":
-                nc.vector.scalar_tensor_tensor(
-                    out=res[:], in0=bank[:], scalar=w_col[:, c : c + 1], in1=off[:, cols], op0=MULT, op1=ADD
-                )
-            elif path == "V2":
+            if path == "V2":
                 for n in (0, W // 2):
                     half = slice(n, n + W // 2)
                     part = slice(W * j + n, W * j + n + W // 2)
@@ -206,81 +204,122 @@ def tile_molecule_embedding_scores_s4_kernel(
                     )
                     nc.sync.dma_start(out=out[P * c : P * (c + 1), part], in_=res[:, half])
                 return
+            if path == "V":
+                nc.vector.scalar_tensor_tensor(
+                    out=res[:], in0=bank[:], scalar=w_col[:, c : c + 1], in1=off[:, cols], op0=MULT, op1=ADD
+                )
             else:
-                tmp = stage.tile([P, W], F32, name="tmp", tag="tmp", bufs=3)
+                tmp = stage.tile([P, W], F32, name="tmp", tag="tmp", bufs=2)
                 nc.scalar.activation(out=tmp[:], in_=bank[:], func=ACT.Copy, scale=w_col[:, c : c + 1])
                 nc.gpsimd.tensor_tensor(out=res[:], in0=tmp[:], in1=off[:, cols], op=ADD)
-            nc.sync.dma_start(out=out[P * c : P * (c + 1), cols], in_=res[:])
+            queue = nc.sync if path == "V" else nc.gpsimd
+            queue.dma_start(out=out[P * c : P * (c + 1), cols], in_=res[:])
 
         banks = {}
-        for d in range(DG):
+        for h in range(2):
             for t in range(4):
-                banks[d, t] = psum.tile([P, W], F32, name="bank", tag="bank")
+                banks[h, t] = psum.tile([P, W], F32, name="bank", tag="bank")
+        for warm_pass in range(3):
+            nc.tensor.matmul_mx(
+                out=banks[0, 0][:],
+                lhsT=m_raw[0][:, 0, 0 : 2 * P].bitcast(FP4X4),
+                lhsT_scale=ms_raw[0][:, 0, 0:P],
+                rhs=m_raw[0][:, 0].bitcast(FP4X4),
+                rhs_scale=ms_raw[0][:, 0],
+                start=True,
+                stop=True,
+            )
         for g in range(KG):
-            permute(g, 0)
-            permute(g, 1)
-            for d in range(DG):
+            words_in_order(g, 0)
+            scales_in_order(g, 0)
+            for h in range(2):
                 for t in range(4):
-                    s1(banks[d, t], 0, d, t, g)
+                    s1(banks[h, t], h, 0, t, g)
+        for g in range(KG):
+            words_in_order(g, 1)
+        for g in range(KG):
+            scales_in_order(g, 1)
         nc.vector.tensor_copy(out=sh_f[:], in_=sh[:])
-        nc.vector.tensor_copy(out=w_f32[:], in_=w_row[:])
         l_split(0, 0)
-        l_split(0, 2)
-        for d in range(DG):
-            for t in range(4):
-                h_out(banks[d, t], 0, d, t, "SV"[t % 2])
-
+        l_split(0, 1)
+        h_out(banks[0, 0], 0, 0, 0, "S")
+        h_out(banks[0, 1], 0, 0, 1, "S")
+        h_out(banks[0, 2], 0, 0, 2, "V")
+        h_out(banks[0, 3], 0, 0, 3, "S")
+        h_out(banks[1, 0], 1, 0, 0, "S")
+        h_out(banks[1, 1], 1, 0, 1, "V")
+        l_split(1, 0)
+        h_out(banks[1, 2], 1, 0, 2, "S")
+        h_out(banks[1, 3], 1, 0, 3, "V")
+        h_interleave(0, 0, 512)
+        s1_whole(0, 1, 0, "S")
+        h_interleave(1, 0, 320)
+        s1_whole(0, 1, 1, "V")
+        l_turn(0, 0, True, "SS")
+        l_turn(0, 1, True, "SS")
+        l_quant(0, 0)
+        l_quant(0, 1)
+        l_turn(1, 0, True, "VV")
+        h_quant(0, 0)
+        h_quant(1, 0)
+        l_split(2, 0)
+        l_split(2, 1)
+        s1_whole(0, 1, 2, "V")
+        s1_whole(0, 1, 3, "V")
+        l_split(1, 1)
+        s1_whole(1, 1, 0, "S")
+        s1_whole(1, 1, 1, "S")
+        h_interleave(0, 1, 320)
+        s1_whole(1, 1, 2, "V")
+        s1_whole(1, 1, 3, "S")
+        l_turn(1, 1, True, "SS")
+        h_quant(0, 1)
+        h_interleave(1, 1, 384)
         bank = psum.tile([P, W], F32, name="bank", tag="bank")
         nc.tensor.transpose(bank[:, 0:P], w_f32[:], ident[:])
         nc.scalar.copy(out=w_col[:], in_=bank[:, 0 : M // P])
-        h_interleave(0, 0)
-        h_interleave(0, 1)
-        h_quant(0, 0)
-        h_quant(0, 1)
-        l_turn(0)
-        l_quant(0, 0)
-        l_quant(0, 1)
-        s1_whole(1, 0, 0)
-        l_split(1, 0)
-        s1_whole(1, 0, 1)
-        l_split(1, 2)
-        s1_whole(1, 0, 2)
-        for i in range(MI):
-            s2(0, 0, i, "V")
-        s1_whole(1, 0, 3)
-        l_turn(1)
-        h_interleave(1, 0)
         l_quant(1, 0)
         l_quant(1, 1)
-        h_quant(1, 0)
-        for t in range(4):
-            s1_whole(1, 1, t)
-        l_split(2, 0)
-        l_split(2, 2)
-        s2(0, 1, 0, "V")
-        h_interleave(1, 1)
-        s2(0, 1, 1, "V")
         h_quant(1, 1)
-        s2(0, 1, 2, "V")
-        s2(0, 1, 3, "V")
-        l_turn(2)
+        l_turn(2, 0, True, "SS")
+        l_turn(2, 1, True, "SS")
         l_split(3, 0)
-        l_split(3, 2)
+        l_split(3, 1)
+        s2(0, 0, 0, "V")
+        s2(0, 0, 1, "V")
+        s2(0, 0, 2, "V")
+        s2(0, 0, 3, "V")
         s2(1, 0, 0, "V")
         s2(1, 0, 1, "V")
         l_quant(2, 0)
-        s2(1, 0, 2, "V")
         l_quant(2, 1)
+        s2(1, 0, 2, "V")
         s2(1, 0, 3, "V")
-        for i in range(MI):
-            s2(1, 1, i, "V")
-        l_turn(3)
+        s2(0, 1, 0, "V")
+        s2(0, 1, 1, "V")
+        s2(0, 1, 2, "V")
+        s2(0, 1, 3, "V")
+        l_turn(3, 0, True, "SS")
+        l_turn(3, 1, True, "SS")
+        s2(1, 1, 0, "V")
+        s2(1, 1, 1, "V")
+        s2(1, 1, 2, "V")
+        s2(1, 1, 3, "V")
         s2(0, 2, 0, "V")
         s2(0, 2, 1, "V")
         l_quant(3, 0)
         l_quant(3, 1)
-        s2(0, 2, 2, "S")
-        s2(0, 2, 3, "V")
-        for h, j in ((1, 2), (0, 3), (1, 3)):
-            for i in range(MI):
-                s2(h, j, i, "S" if i == 1 else "V2" if (h, j, i) == (1, 3, 3) else "V")
+        s2(0, 2, 2, "V")
+        s2(0, 2, 3, "S")
+        s2(1, 2, 0, "V")
+        s2(1, 2, 1, "S")
+        s2(1, 2, 2, "V")
+        s2(1, 2, 3, "V")
+        s2(0, 3, 0, "V")
+        s2(0, 3, 1, "V")
+        s2(0, 3, 2, "V")
+        s2(0, 3, 3, "V")
+        s2(1, 3, 0, "V")
+        s2(1, 3, 1, "V")
+        s2(1, 3, 2, "V")
+        s2(1, 3, 3, "V2")

from contextlib import ExitStack

import concourse.mybir as mybir
from concourse.masks import make_identity

M, K, D, N = 1024, 2048, 1024, 2048
FLOPS = 2 * M * K * D + 2 * M * D * N

F32 = mybir.dt.float32
BF16 = mybir.dt.bfloat16
I32 = mybir.dt.int32
U32 = mybir.dt.uint32
U8 = mybir.dt.uint8
FP4X4 = mybir.dt.float4_e2m1fn_x4
FP8X4 = mybir.dt.float8_e4m3fn_x4
ADD = mybir.AluOpType.add
MULT = mybir.AluOpType.mult
MAX = mybir.AluOpType.max
ACT = mybir.ActivationFunctionType

P = 128
KG = K // 512
DG = D // 512
W = 512
MI = W // P
NJ = N // W


def tile_molecule_embedding_scores_s4_kernel(
    tc, fp_words, fp_scales, metric_words, metric_scales, shift, library, weight, offset, out
):
    nc = tc.nc
    with ExitStack() as ctx:
        keep = ctx.enter_context(tc.tile_pool(name="keep", bufs=1))
        stage = ctx.enter_context(tc.tile_pool(name="stage", bufs=12))
        psum = ctx.enter_context(tc.psum_pool(name="psum", bufs=8))
        ctx.enter_context(tc.manual_schedule())

        m_raw = [keep.tile([P, KG, D], U8, align_bytes=64, name=f"m_raw{d}") for d in range(DG)]
        m_cod = [keep.tile([P, KG, 4, 2 * P], U8, align_bytes=64, name=f"m_cod{d}") for d in range(DG)]
        ms_raw = [keep.tile([P, KG, W], U8, align_bytes=64, name=f"ms_raw{d}") for d in range(DG)]
        ms_cod = [keep.tile([P, KG, 4, P], U8, align_bytes=64, name=f"ms_cod{d}") for d in range(DG)]
        f_cod = keep.tile([P, KG, 2 * M], U8, align_bytes=64, name="f_cod")
        f_scl = keep.tile([P, KG, M], U8, align_bytes=64, name="f_scl")
        sh = keep.tile([P, DG, 4], BF16, name="sh")
        sh_f = keep.tile([P, DG, 4], F32, name="sh_f")
        w_row = keep.tile([P, P], BF16, name="w_row")
        w_f32 = keep.tile([P, P], F32, name="w_f32")
        w_col = keep.tile([P, M // P], F32, name="w_col")
        off = keep.tile([P, N], BF16, name="off")
        ident = keep.tile([P, P], F32, name="ident")
        warm = keep.tile([P, 1], F32, name="warm")

        l_raw = [[keep.tile([P, 2, D], BF16, align_bytes=64, name=f"l_raw{j}{b}") for b in range(2)] for j in range(NJ)]
        l_spl = [[keep.tile([P, 2, D // 2], F32, align_bytes=64, name=f"l_spl{j}{b}") for b in range(2)] for j in range(NJ)]
        l_grp = {}
        l_cod = {}
        l_scl = {}
        for j in range(NJ):
            for g in range(DG):
                l_grp[j, g] = keep.tile([P, 4 * W], BF16, align_bytes=64, name=f"l_grp{j}{g}")
                l_cod[j, g] = keep.tile([P, W], U32, align_bytes=64, name=f"l_cod{j}{g}")
                l_scl[j, g] = keep.tile([P, W], U8, align_bytes=64, name=f"l_scl{j}{g}")
        h_raw = {}
        h_grp = {}
        h_cod = {}
        h_scl = {}
        for h in range(2):
            for g in range(DG):
                h_raw[h, g] = keep.tile([P, 4, W], BF16, align_bytes=64, name=f"h_raw{h}{g}")
                h_grp[h, g] = keep.tile([P, 4 * W], BF16, align_bytes=64, name=f"h_grp{h}{g}")
                h_cod[h, g] = keep.tile([P, W], U32, align_bytes=64, name=f"h_cod{h}{g}")
                h_scl[h, g] = keep.tile([P, W], U8, align_bytes=64, name=f"h_scl{h}{g}")

        def scales(dst, src):
            rows = src.rearrange("g (q r) n -> r q g n", r=4)
            for r in range(4):
                nc.sync.dma_start(out=dst[:].bitcast(I32)[r:P:32], in_=rows[r])

        mi = metric_scales.bitcast(I32)
        mi = [mi[:, :, W // 4 * d : W // 4 * (d + 1)] for d in range(DG)]

        fa = fp_words.rearrange("g p w -> p g w")
        ma = metric_words.rearrange("g p (d w) -> d p g w", d=DG)
        lib = library.rearrange("(j b a p) k -> j b p a k", b=2, a=2, p=P)
        nc.gpsimd.dma_start(out=f_cod[:].bitcast(I32)[:, 0], in_=fa.bitcast(I32)[:, 0])
        nc.vector.memset(ms_raw[0][:].bitcast(I32), 0)
        nc.vector.memset(f_scl[:].bitcast(I32), 0)
        nc.vector.memset(ms_raw[1][:].bitcast(I32), 0)
        nc.vector.memset(warm[:], 0.0)
        nc.scalar.activation(out=warm[:], in_=warm[:], func=ACT.Relu)
        make_identity(nc, ident[:])
        nc.gpsimd.memset(w_row[:], 0.0)
        nc.sync.dma_start(out=m_raw[0][:, 0], in_=ma[0][:, 0])
        scales(ms_raw[0], mi[0])
        scales(f_scl, fp_scales.bitcast(I32))
        nc.sync.dma_start(out=m_raw[0][:, 1], in_=ma[0][:, 1])
        nc.sync.dma_start(out=f_cod[:, 1], in_=fa[:, 1])
        nc.sync.dma_start(out=m_raw[0][:, 2:4], in_=ma[0][:, 2:4])
        nc.sync.dma_start(out=f_cod[:, 2:4], in_=fa[:, 2:4])
        nc.sync.dma_start(out=m_raw[1][:], in_=ma[1])
        scales(ms_raw[1], mi[1])
        nc.sync.dma_start(out=sh[:], in_=shift.rearrange("(g p t) -> p g t", p=P, t=4))
        nc.sync.dma_start(out=w_row[0 : M // P, :], in_=weight.rearrange("(c p) -> c p", p=P))
        for j in range(NJ):
            for b in range(2):
                nc.sync.dma_start(out=l_raw[j][b][:], in_=lib[j, b])
        nc.sync.dma_start(out=off[:], in_=offset.partition_broadcast(P))

        nc.gpsimd.tensor_copy(out=w_f32[:], in_=w_row[:])

        def l_split(j, b):
            nc.scalar.copy(
                out=l_spl[j][b][:].rearrange("p a (g u q) -> p (a g) u q", g=DG, u=2),
                in_=l_raw[j][b][:].bitcast(F32).rearrange("p a (g q u) -> p (a g) u q", g=DG, u=2),
            )

        def words_in_order(g, d):
            nc.vector.tensor_copy(
                out=m_cod[d][:, g].rearrange("p t (q b) -> p t q b", b=2),
                in_=m_raw[d][:, g].rearrange("p (q t b) -> p t q b", t=4, b=2),
            )

        def scales_in_order(g, d):
            nc.vector.tensor_copy(out=ms_cod[d][:, g], in_=ms_raw[d][:, g].rearrange("p (q t) -> p t q", t=4))

        def s1(bank, h, d, t, g):
            nc.tensor.matmul_mx(
                out=bank[:],
                lhsT=m_cod[d][:, g, t, :].bitcast(FP4X4),
                lhsT_scale=ms_cod[d][:, g, t, :],
                rhs=f_cod[:, g, 1024 * h : 1024 * (h + 1)].bitcast(FP4X4),
                rhs_scale=f_scl[:, g, 512 * h : 512 * (h + 1)],
                start=(g == 0),
                stop=(g == KG - 1),
            )

        def h_out(bank, h, d, t, eng):
            if eng == "S":
                nc.scalar.activation(out=h_raw[h, d][:, t, :], in_=bank[:], func=ACT.Relu, bias=sh[:, d, t : t + 1])
            else:
                nc.vector.tensor_scalar(
                    out=h_raw[h, d][:, t, :], in0=bank[:], scalar1=sh_f[:, d, t : t + 1], scalar2=0.0, op0=ADD, op1=MAX
                )

        def h_interleave(h, d, vector_cols):
            for eng, cols in ((nc.vector.tensor_copy, slice(0, vector_cols)), (nc.scalar.copy, slice(vector_cols, W))):
                if cols.start < cols.stop:
                    eng(
                        out=h_grp[h, d][:, 4 * cols.start : 4 * cols.stop].rearrange("p (c i t) -> p c t i", i=4, t=4),
                        in_=h_raw[h, d][:, :, cols].rearrange("p t (c i) -> p c t i", i=4),
                    )

        def h_quant(h, d):
            nc.vector.quantize_mx(out=h_cod[h, d][:].bitcast(FP8X4), scales=h_scl[h, d][:], in_=h_grp[h, d][:])

        def l_quant(j, g):
            nc.vector.quantize_mx(out=l_cod[j, g][:].bitcast(FP8X4), scales=l_scl[j, g][:], in_=l_grp[j, g][:])

        def s1_whole(h, d, t, eng):
            bank = psum.tile([P, W], F32, name="bank", tag="bank")
            for g in range(KG):
                s1(bank, h, d, t, g)
            h_out(bank, h, d, t, eng)

        def l_turn(j, b, split, engs):
            for g in range(DG):
                bank = psum.tile([P, W], F32, name="bank", tag="bank")
                for a in range(2):
                    for u in range(2):
                        if split:
                            words = l_spl[j][b][:, a, (2 * g + u) * P : (2 * g + u + 1) * P]
                        else:
                            words = l_raw[j][b][:, a, :].bitcast(F32)[:, 256 * g + u : 256 * (g + 1) : 2]
                        nc.tensor.transpose(bank[:, (2 * a + u) * P : (2 * a + u + 1) * P], words, ident[:])
                dst = l_grp[j, g][:].bitcast(F32)[:, 512 * b : 512 * (b + 1)].rearrange("p (a r u) -> p a r u", a=2, u=2)
                src = bank[:].rearrange("p (a u r) -> p a r u", a=2, u=2)
                if engs[g] == "S":
                    nc.scalar.copy(out=dst, in_=src)
                else:
                    nc.vector.tensor_copy(out=dst, in_=src)

        def s2(h, j, i, path="V"):
            bank = psum.tile([P, W], F32, name="bank", tag="bank")
            for g in range(DG):
                nc.tensor.matmul_mx(
                    out=bank[:],
                    lhsT=h_cod[h, g][:, P * i : P * (i + 1)].bitcast(FP8X4),
                    lhsT_scale=h_scl[h, g][:, P * i : P * (i + 1)],
                    rhs=l_cod[j, g][:].bitcast(FP8X4),
                    rhs_scale=l_scl[j, g][:],
                    start=(g == 0),
                    stop=(g == DG - 1),
                )
            res = stage.tile([P, W], F32, name="res", tag="res")
            c = MI * h + i
            cols = slice(W * j, W * (j + 1))
            if path == "V2":
                for n in (0, W // 2):
                    half = slice(n, n + W // 2)
                    part = slice(W * j + n, W * j + n + W // 2)
                    nc.vector.scalar_tensor_tensor(
                        out=res[:, half], in0=bank[:, half], scalar=w_col[:, c : c + 1], in1=off[:, part], op0=MULT, op1=ADD
                    )
                    nc.sync.dma_start(out=out[P * c : P * (c + 1), part], in_=res[:, half])
                return
            if path == "V":
                nc.vector.scalar_tensor_tensor(
                    out=res[:], in0=bank[:], scalar=w_col[:, c : c + 1], in1=off[:, cols], op0=MULT, op1=ADD
                )
            else:
                tmp = stage.tile([P, W], F32, name="tmp", tag="tmp", bufs=2)
                nc.scalar.activation(out=tmp[:], in_=bank[:], func=ACT.Copy, scale=w_col[:, c : c + 1])
                nc.gpsimd.tensor_tensor(out=res[:], in0=tmp[:], in1=off[:, cols], op=ADD)
            queue = nc.sync if path == "V" else nc.gpsimd
            queue.dma_start(out=out[P * c : P * (c + 1), cols], in_=res[:])

        banks = {}
        for h in range(2):
            for t in range(4):
                banks[h, t] = psum.tile([P, W], F32, name="bank", tag="bank")
        for warm_pass in range(3):
            nc.tensor.matmul_mx(
                out=banks[0, 0][:],
                lhsT=m_raw[0][:, 0, 0 : 2 * P].bitcast(FP4X4),
                lhsT_scale=ms_raw[0][:, 0, 0:P],
                rhs=m_raw[0][:, 0].bitcast(FP4X4),
                rhs_scale=ms_raw[0][:, 0],
                start=True,
                stop=True,
            )
        for g in range(KG):
            words_in_order(g, 0)
            scales_in_order(g, 0)
            for h in range(2):
                for t in range(4):
                    s1(banks[h, t], h, 0, t, g)
        for g in range(KG):
            words_in_order(g, 1)
        for g in range(KG):
            scales_in_order(g, 1)
        nc.vector.tensor_copy(out=sh_f[:], in_=sh[:])
        l_split(0, 0)
        l_split(0, 1)
        h_out(banks[0, 0], 0, 0, 0, "S")
        h_out(banks[0, 1], 0, 0, 1, "S")
        h_out(banks[0, 2], 0, 0, 2, "V")
        h_out(banks[0, 3], 0, 0, 3, "S")
        h_out(banks[1, 0], 1, 0, 0, "S")
        h_out(banks[1, 1], 1, 0, 1, "V")
        l_split(1, 0)
        h_out(banks[1, 2], 1, 0, 2, "S")
        h_out(banks[1, 3], 1, 0, 3, "V")
        h_interleave(0, 0, 512)
        s1_whole(0, 1, 0, "S")
        h_interleave(1, 0, 320)
        s1_whole(0, 1, 1, "V")
        l_turn(0, 0, True, "SS")
        l_turn(0, 1, True, "SS")
        l_quant(0, 0)
        l_quant(0, 1)
        l_turn(1, 0, True, "VV")
        h_quant(0, 0)
        h_quant(1, 0)
        l_split(2, 0)
        l_split(2, 1)
        s1_whole(0, 1, 2, "V")
        s1_whole(0, 1, 3, "V")
        l_split(1, 1)
        s1_whole(1, 1, 0, "S")
        s1_whole(1, 1, 1, "S")
        h_interleave(0, 1, 320)
        s1_whole(1, 1, 2, "V")
        s1_whole(1, 1, 3, "S")
        l_turn(1, 1, True, "SS")
        h_quant(0, 1)
        h_interleave(1, 1, 384)
        bank = psum.tile([P, W], F32, name="bank", tag="bank")
        nc.tensor.transpose(bank[:, 0:P], w_f32[:], ident[:])
        nc.scalar.copy(out=w_col[:], in_=bank[:, 0 : M // P])
        l_quant(1, 0)
        l_quant(1, 1)
        h_quant(1, 1)
        l_turn(2, 0, True, "SS")
        l_turn(2, 1, True, "SS")
        l_split(3, 0)
        l_split(3, 1)
        s2(0, 0, 0, "V")
        s2(0, 0, 1, "V")
        s2(0, 0, 2, "V")
        s2(0, 0, 3, "V")
        s2(1, 0, 0, "V")
        s2(1, 0, 1, "V")
        l_quant(2, 0)
        l_quant(2, 1)
        s2(1, 0, 2, "V")
        s2(1, 0, 3, "V")
        s2(0, 1, 0, "V")
        s2(0, 1, 1, "V")
        s2(0, 1, 2, "V")
        s2(0, 1, 3, "V")
        l_turn(3, 0, True, "SS")
        l_turn(3, 1, True, "SS")
        s2(1, 1, 0, "V")
        s2(1, 1, 1, "V")
        s2(1, 1, 2, "V")
        s2(1, 1, 3, "V")
        s2(0, 2, 0, "V")
        s2(0, 2, 1, "V")
        l_quant(3, 0)
        l_quant(3, 1)
        s2(0, 2, 2, "V")
        s2(0, 2, 3, "S")
        s2(1, 2, 0, "V")
        s2(1, 2, 1, "S")
        s2(1, 2, 2, "V")
        s2(1, 2, 3, "V")
        s2(0, 3, 0, "V")
        s2(0, 3, 1, "V")
        s2(0, 3, 2, "V")
        s2(0, 3, 3, "V")
        s2(1, 3, 0, "V")
        s2(1, 3, 1, "V")
        s2(1, 3, 2, "V")
        s2(1, 3, 3, "V2")
